import numpy as np
import ml_dtypes


def mxq(x, axis, fmt="e4m3"):
    dtype, down = {"e4m3": (ml_dtypes.float8_e4m3fn, 7), "e5m2": (ml_dtypes.float8_e5m2, 14)}[fmt]
    v = np.moveaxis(np.asarray(x, np.float32).astype(ml_dtypes.bfloat16).astype(np.float64), axis, -1)
    blocks = v.reshape(v.shape[:-1] + (-1, 32))
    amax = np.abs(blocks).max(-1, keepdims=True)
    byte = np.maximum(np.where(amax > 0, np.frexp(amax)[1] - 1 + 127, 0) - down, 1)
    scale = np.exp2(byte - 127.0)
    codes = (blocks / scale).astype(np.float32).astype(dtype).astype(np.float64)
    return np.moveaxis((codes * scale).reshape(v.shape), -1, axis)


WIDE = False


def mx_kscale(k):
    if not WIDE:
        return np.ones(k)
    levels = np.array([10, -10, 5, -5, 0])
    if k % 512:
        return np.exp2(np.random.permutation(np.resize(levels, k // 32))).repeat(32)
    a = np.empty((k // 512, 16))
    for p in range(k // 512):
        a[p, :8] = np.random.permutation(np.resize(levels, 8))
        for g in range(8):
            far = levels[np.abs(levels - a[p, g]) >= 10]
            a[p, g + 8] = far[np.random.randint(len(far))]
    return np.exp2(a.ravel()).repeat(32)


def f64(x):
    return np.asarray(x).astype(np.float64)


def striped(idx):
    return np.tile(idx.reshape(-1, 16).T, (8, 1)).astype(np.uint16)


def unstriped(offs):
    return offs[:16].T.reshape(-1).astype(np.int64)


def striped8(idx):
    return np.concatenate([x.reshape(-1, 16).T for x in idx]).astype(np.uint16)


def runs(offs, k):
    lists = np.stack([offs[16 * r : 16 * r + 16].T.reshape(-1) for r in range(8)]).astype(np.int64)
    return lists[np.arange(k) % 512 // 64]


def pack_weight(w):
    k, n = w.shape
    w = f64(np.asarray(w, np.float32).astype(ml_dtypes.bfloat16)).reshape(k // 32, 32, n)
    amax = np.abs(w).max(1)
    byte = np.clip(np.where(amax > 0, np.frexp(amax)[1] - 1 + 127 - 7, 1), 1, 254)
    scaled = (w * np.exp2(127.0 - byte)[:, None, :]).reshape(k, n).astype(np.float32)
    words = np.ascontiguousarray(scaled.reshape(k // 512, 128, 4, n).transpose(0, 1, 3, 2)).astype(ml_dtypes.float8_e4m3fn).view(np.uint8)
    return words, np.ascontiguousarray(byte.astype(np.uint8).reshape(k // 512, 16, n))


def unpack_weight(words, scales):
    g, p, n, _ = words.shape
    vals = np.ascontiguousarray(words).view(ml_dtypes.float8_e4m3fn).astype(np.float64) * np.repeat(np.exp2(scales.astype(np.float64) - 127.0), 8, axis=1)[..., None]
    return vals.transpose(0, 1, 3, 2).reshape(g * 512, n)


def silu(v):
    return v / (1.0 + np.exp(-np.maximum(v, -700.0)))


K, T, S, N = 512, 2048, 512, 256


def setup_inputs():
    n = np.random.standard_normal
    s = mx_kscale(K)[:, None]
    packed_xT = pack_weight(n((K, T)) * s)
    return {
        "x_words": packed_xT[0],
        "x_scales": packed_xT[1],
        "w1": (n((K, N)) / np.sqrt(K) / s).astype(np.float32),
        "w2": (n((K, N)) / np.sqrt(K) / s).astype(np.float32),
        "offs": striped8(np.stack([np.random.permutation(T)[:S] for _ in range(8)])),
        "own": striped(np.random.permutation(T)[:S]),
    }


def reference(x_words, x_scales, w1, w2, offs, own):
    xq = unpack_weight(x_words, x_scales)[np.arange(K)[:, None], runs(offs, K)]
    y = mxq(f64(w1), 0, "e4m3").T @ xq
    xown = unpack_weight(x_words, x_scales)[:, unstriped(own)]
    e = mxq(f64(w2), 0, "e4m3").T @ xown
    return silu(y) * e

@@ -1,0 +1,116 @@
+from contextlib import ExitStack
+
+import concourse.mybir as mybir
+
+K, T, S, N = 512, 2048, 512, 256
+FLOPS = 2 * 2 * K * N * S
+
+F32 = mybir.dt.float32
+BF16 = mybir.dt.bfloat16
+I32 = mybir.dt.int32
+U32 = mybir.dt.uint32
+U16 = mybir.dt.uint16
+U8 = mybir.dt.uint8
+FP8X4 = mybir.dt.float8_e4m3fn_x4
+SILU = mybir.ActivationFunctionType.Silu
+MULT = mybir.AluOpType.mult
+
+P = 128
+PACK = 4
+M_TILE = 128
+HALF = S // 2
+
+
+def tile_picked_phmix_silu_p_kernel(tc, x_words, x_scales, w1, w2, offs, own, out):
+    nc = tc.nc
+    m_tiles = N // M_TILE
+    with ExitStack() as ctx:
+        keep = ctx.enter_context(tc.tile_pool(name="keep", bufs=1))
+        psum = ctx.enter_context(tc.psum_pool(name="psum", bufs=1))
+
+        offs_sb = keep.tile([P, S // 16], U16, name="offs_sb")
+        own_sb = keep.tile([P, S // 16], U16, name="own_sb")
+        nc.sync.dma_start(offs_sb[:], offs)
+        nc.sync.dma_start(own_sb[:], own)
+
+        scale_table = keep.tile([P, T], U8, name="scale_table", align_bytes=64)
+        head_plane = keep.tile([P, S], U8, name="head_plane", align_bytes=64)
+        nc.vector.memset(scale_table[:].bitcast(I32), 0)
+        warm = keep.tile([P, 8], F32, name="warm")
+        nc.vector.memset(warm[:, 0:1], 0.0)
+        nc.vector.memset(head_plane[:].bitcast(I32), 0)
+        rows = x_scales[0].bitcast(I32)
+        table_rows = scale_table[:].bitcast(I32)
+        for j in range(2):
+            nc.scalar.dma_start(table_rows[j:P:16, :], rows[j:16:2, :])
+        for j in range(2, 4):
+            nc.scalar.dma_start(table_rows[j:P:32, :], rows[j:16:4, :])
+        nc.scalar.activation(warm[:, 1:2], warm[:, 0:1], SILU)
+
+        raw = keep.tile([P, PACK, N], F32, name="raw")
+        nc.sync.dma_start(raw[:], w1.rearrange("(p j) n -> p j n", j=PACK))
+        word_table = keep.tile([P, T], U32, name="word_table", align_bytes=64)
+        nc.sync.dma_start(word_table[:].bitcast(I32), x_words[0].rearrange("p c r -> p (c r)").bitcast(I32))
+
+        def cast(name, mt):
+            grouped = keep.tile([P, M_TILE, PACK], BF16, name=name, align_bytes=64)
+            src = raw[:, :, mt * M_TILE : (mt + 1) * M_TILE]
+            nc.scalar.copy(grouped[:].rearrange("p (c i) t -> p c t i", i=4), src.rearrange("p t (c i) -> p c t i", i=4))
+            return grouped
+
+        def quantise(name, grouped):
+            codes = keep.tile([P, M_TILE], U32, name=name + "_codes", align_bytes=64)
+            plane = keep.tile([P, M_TILE], U8, name=name + "_plane", align_bytes=64)
+            nc.vector.quantize_mx(out=codes[:].bitcast(FP8X4), scales=plane[:], in_=grouped[:].rearrange("p c t -> p (c t)"))
+            return codes, plane
+
+        head_bytes = keep.tile([P, S], U8, name="head_bytes", align_bytes=64)
+        nc.vector.tensor_copy(head_bytes[:], scale_table[:].indirect(offs_sb[:]))
+        own_plane = keep.tile([P, S], U8, name="own_plane", align_bytes=64)
+        nc.vector.tensor_copy(own_plane[:], scale_table[:].indirect(own_sb[:]))
+
+        w1_grouped = [cast("w1g%d" % mt, mt) for mt in range(m_tiles)]
+        w2_rows = w2.rearrange("(p j) n -> p j n", j=PACK)
+        for mt in range(m_tiles):
+            cols = slice(mt * M_TILE, (mt + 1) * M_TILE)
+            nc.sync.dma_start(raw[:, :, cols], w2_rows[:, :, cols])
+
+        src_rows = head_bytes[:].bitcast(I32)
+        dst_rows = head_plane[:].bitcast(I32)
+        for j in range(4):
+            first = 16 * (j // 2) + j % 2
+            nc.scalar.dma_start(dst_rows[j:P:32, :], src_rows[first:P:32, :])
+
+        w1_q = [quantise("w1q%d" % mt, w1_grouped[mt]) for mt in range(m_tiles)]
+
+        head_words = keep.tile([P, S], U32, name="head_words", align_bytes=64)
+        nc.vector.tensor_copy(head_words[:], word_table[:].indirect(offs_sb[:]))
+
+        w2_grouped = [cast("w2g%d" % mt, mt) for mt in range(m_tiles)]
+
+        gates = []
+        for mt in range(m_tiles):
+            y = psum.tile([P, S], F32, name="y%d" % mt)
+            nc.tensor.matmul_mx(out=y[:], lhsT=w1_q[mt][0][:].bitcast(FP8X4), lhsT_scale=w1_q[mt][1][:],
+                                rhs=head_words[:].bitcast(FP8X4), rhs_scale=head_plane[:], start=True, stop=True)
+            gate = keep.tile([P, S], F32, name="gate%d" % mt)
+            nc.scalar.activation(gate[:], y[:], SILU)
+            gates.append(gate)
+
+        own_words = []
+        for h in range(2):
+            words = keep.tile([P, HALF], U32, name="own_words%d" % h, align_bytes=64)
+            nc.vector.tensor_copy(words[:], word_table[:].indirect(own_sb[:, h * HALF // 16 : (h + 1) * HALF // 16]))
+            own_words.append(words)
+        w2_q = [quantise("w2q%d" % mt, w2_grouped[mt]) for mt in range(m_tiles)]
+
+        for mt in range(m_tiles):
+            for h in range(2):
+                cols = slice(h * HALF, (h + 1) * HALF)
+                e = psum.tile([P, HALF], F32, name="e%d_%d" % (mt, h))
+                nc.tensor.matmul_mx(out=e[:], lhsT=w2_q[mt][0][:].bitcast(FP8X4), lhsT_scale=w2_q[mt][1][:],
+                                    rhs=own_words[h][:].bitcast(FP8X4), rhs_scale=own_plane[:, cols], start=True, stop=True)
+                res = keep.tile([P, HALF], F32, name="res%d_%d" % (mt, h))
+                nc.vector.tensor_tensor(res[:], e[:], gates[mt][:, cols], MULT)
+                queue = nc.sync if h == 0 else nc.scalar
+                queue.dma_start(out[mt * M_TILE : (mt + 1) * M_TILE, cols], res[:])

@@ -26,91 +26,89 @@ def tile_picked_phmix_silu_p_kernel(tc, x_words, x_scales, w1, w2, offs, own, ou
     m_tiles = N // M_TILE
     with ExitStack() as ctx:
         keep = ctx.enter_context(tc.tile_pool(name="keep", bufs=1))
+        reuse = ctx.enter_context(tc.tile_pool(name="reuse", bufs=1))
         psum = ctx.enter_context(tc.psum_pool(name="psum", bufs=1))
 
         offs_sb = keep.tile([P, S // 16], U16, name="offs_sb")
         own_sb = keep.tile([P, S // 16], U16, name="own_sb")
-        nc.sync.dma_start(offs_sb[:], offs)
-        nc.sync.dma_start(own_sb[:], own)
-
         scale_table = keep.tile([P, T], U8, name="scale_table", align_bytes=64)
-        head_plane = keep.tile([P, S], U8, name="head_plane", align_bytes=64)
-        nc.vector.memset(scale_table[:].bitcast(I32), 0)
+        word_table = keep.tile([P, T], U32, name="word_table", align_bytes=64)
+        w1_raw = reuse.tile([P, PACK, N], F32, name="w1_raw", offset=8192, align_bytes=64)
+        w2_raw = [keep.tile([P, PACK, M_TILE], F32, name="w2_raw0"),
+                  reuse.tile([P, PACK, M_TILE], F32, name="w2_raw1", offset=0, align_bytes=64)]
+        nc.sync.dma_start(offs_sb[:], offs)
+        nc.sync.dma_start(scale_table[:].bitcast(I32), x_scales[0].bitcast(I32).unsqueeze(1).broadcast_to([16, 8, T // 4]))
+        nc.sync.dma_start(own_sb[:], own)
+        nc.sync.dma_start(w1_raw[:], w1.rearrange("(p j) n -> p j n", j=PACK))
+        nc.sync.dma_start(word_table[:].bitcast(I32), x_words[0].rearrange("p c r -> p (c r)").bitcast(I32))
+        w2_rows = w2.rearrange("(p j) n -> p j n", j=PACK)
+        for mt in range(m_tiles):
+            nc.sync.dma_start(w2_raw[mt][:], w2_rows[:, :, mt * M_TILE : (mt + 1) * M_TILE])
+
         warm = keep.tile([P, 8], F32, name="warm")
         nc.vector.memset(warm[:, 0:1], 0.0)
-        nc.vector.memset(head_plane[:].bitcast(I32), 0)
-        rows = x_scales[0].bitcast(I32)
-        table_rows = scale_table[:].bitcast(I32)
-        for j in range(2):
-            nc.scalar.dma_start(table_rows[j:P:16, :], rows[j:16:2, :])
-        for j in range(2, 4):
-            nc.scalar.dma_start(table_rows[j:P:32, :], rows[j:16:4, :])
         nc.scalar.activation(warm[:, 1:2], warm[:, 0:1], SILU)
 
-        raw = keep.tile([P, PACK, N], F32, name="raw")
-        nc.sync.dma_start(raw[:], w1.rearrange("(p j) n -> p j n", j=PACK))
-        word_table = keep.tile([P, T], U32, name="word_table", align_bytes=64)
-        nc.sync.dma_start(word_table[:].bitcast(I32), x_words[0].rearrange("p c r -> p (c r)").bitcast(I32))
-
-        def cast(name, mt):
-            grouped = keep.tile([P, M_TILE, PACK], BF16, name=name, align_bytes=64)
-            src = raw[:, :, mt * M_TILE : (mt + 1) * M_TILE]
-            nc.scalar.copy(grouped[:].rearrange("p (c i) t -> p c t i", i=4), src.rearrange("p t (c i) -> p c t i", i=4))
+        def cast(name, raw):
+            grouped = keep.tile([P, raw.shape[2], PACK], BF16, name=name, align_bytes=64)
+            nc.scalar.copy(grouped[:].rearrange("p (c i) t -> p c t i", i=4), raw[:].rearrange("p t (c i) -> p c t i", i=4))
             return grouped
 
         def quantise(name, grouped):
-            codes = keep.tile([P, M_TILE], U32, name=name + "_codes", align_bytes=64)
-            plane = keep.tile([P, M_TILE], U8, name=name + "_plane", align_bytes=64)
+            codes = keep.tile([P, grouped.shape[1]], U32, name=name + "_codes", align_bytes=64)
+            plane = keep.tile([P, grouped.shape[1]], U8, name=name + "_plane", align_bytes=64)
             nc.vector.quantize_mx(out=codes[:].bitcast(FP8X4), scales=plane[:], in_=grouped[:].rearrange("p c t -> p (c t)"))
             return codes, plane
 
-        head_bytes = keep.tile([P, S], U8, name="head_bytes", align_bytes=64)
-        nc.vector.tensor_copy(head_bytes[:], scale_table[:].indirect(offs_sb[:]))
-        own_plane = keep.tile([P, S], U8, name="own_plane", align_bytes=64)
-        nc.vector.tensor_copy(own_plane[:], scale_table[:].indirect(own_sb[:]))
+        def pick_bytes(name, offsets):
+            picked = keep.tile([P, S], U8, name=name, align_bytes=64)
+            nc.vector.tensor_copy(picked[:], scale_table[:].indirect(offsets[:]))
+            return picked
 
-        w1_grouped = [cast("w1g%d" % mt, mt) for mt in range(m_tiles)]
-        w2_rows = w2.rearrange("(p j) n -> p j n", j=PACK)
-        for mt in range(m_tiles):
-            cols = slice(mt * M_TILE, (mt + 1) * M_TILE)
-            nc.sync.dma_start(raw[:, :, cols], w2_rows[:, :, cols])
+        def place_rows(plane, picked):
+            src_rows = picked[:].bitcast(I32)
+            dst_rows = plane[:].bitcast(I32)
+            nc.vector.tensor_copy(dst_rows, src_rows)
+            for j in range(1, 4):
+                nc.sync.dma_start(dst_rows[j:P:32, :], src_rows[8 * j : P : 32, :])
 
-        src_rows = head_bytes[:].bitcast(I32)
-        dst_rows = head_plane[:].bitcast(I32)
-        for j in range(4):
-            first = 16 * (j // 2) + j % 2
-            nc.scalar.dma_start(dst_rows[j:P:32, :], src_rows[first:P:32, :])
+        def pick_words(words, offsets, h):
+            nc.vector.tensor_copy(words[:], word_table[:].indirect(offsets[:, h * HALF // 16 : (h + 1) * HALF // 16]))
 
-        w1_q = [quantise("w1q%d" % mt, w1_grouped[mt]) for mt in range(m_tiles)]
+        head_plane = keep.tile([P, S], U8, name="head_plane", align_bytes=64)
+        place_rows(head_plane, pick_bytes("head_bytes", offs_sb))
+        own_bytes = pick_bytes("own_bytes", own_sb)
+        w1_codes, w1_plane = quantise("w1", cast("w1_grouped", w1_raw))
+        own_plane = reuse.tile([P, S], U8, name="own_plane", offset=8192, align_bytes=64)
+        place_rows(own_plane, own_bytes)
 
-        head_words = keep.tile([P, S], U32, name="head_words", align_bytes=64)
-        nc.vector.tensor_copy(head_words[:], word_table[:].indirect(offs_sb[:]))
-
-        w2_grouped = [cast("w2g%d" % mt, mt) for mt in range(m_tiles)]
-
-        gates = []
-        for mt in range(m_tiles):
-            y = psum.tile([P, S], F32, name="y%d" % mt)
-            nc.tensor.matmul_mx(out=y[:], lhsT=w1_q[mt][0][:].bitcast(FP8X4), lhsT_scale=w1_q[mt][1][:],
-                                rhs=head_words[:].bitcast(FP8X4), rhs_scale=head_plane[:], start=True, stop=True)
-            gate = keep.tile([P, S], F32, name="gate%d" % mt)
-            nc.scalar.activation(gate[:], y[:], SILU)
-            gates.append(gate)
-
-        own_words = []
+        head_words = [keep.tile([P, HALF], U32, name="head_words%d" % h, align_bytes=64) for h in range(2)]
         for h in range(2):
-            words = keep.tile([P, HALF], U32, name="own_words%d" % h, align_bytes=64)
-            nc.vector.tensor_copy(words[:], word_table[:].indirect(own_sb[:, h * HALF // 16 : (h + 1) * HALF // 16]))
-            own_words.append(words)
-        w2_q = [quantise("w2q%d" % mt, w2_grouped[mt]) for mt in range(m_tiles)]
+            pick_words(head_words[h], offs_sb, h)
+        own_words = [keep.tile([P, HALF], U32, name="own_words0", align_bytes=64)]
+        pick_words(own_words[0], own_sb, 0)
 
-        for mt in range(m_tiles):
-            for h in range(2):
-                cols = slice(h * HALF, (h + 1) * HALF)
+        w2_q = [quantise("w2_%d" % mt, cast("w2_grouped%d" % mt, w2_raw[mt])) for mt in range(m_tiles)]
+
+        own_words.append(reuse.tile([P, HALF], U32, name="own_words1", offset=0, align_bytes=64))
+        pick_words(own_words[1], own_sb, 1)
+
+        gate = reuse.tile([P, 2, m_tiles, HALF], F32, name="gate", offset=HALF * 4, align_bytes=64)
+        for h in range(2):
+            cols = slice(h * HALF, (h + 1) * HALF)
+            for mt in range(m_tiles):
+                chans = slice(mt * M_TILE, (mt + 1) * M_TILE)
+                y = psum.tile([P, HALF], F32, name="y%d_%d" % (mt, h))
+                nc.tensor.matmul_mx(out=y[:], lhsT=w1_codes[:, chans].bitcast(FP8X4), lhsT_scale=w1_plane[:, chans],
+                                    rhs=head_words[h][:].bitcast(FP8X4), rhs_scale=head_plane[:, cols], start=True, stop=True)
+                nc.scalar.activation(gate[:, h, mt, :], y[:], SILU)
+
+        for h in range(2):
+            cols = slice(h * HALF, (h + 1) * HALF)
+            for mt in range(m_tiles):
                 e = psum.tile([P, HALF], F32, name="e%d_%d" % (mt, h))
                 nc.tensor.matmul_mx(out=e[:], lhsT=w2_q[mt][0][:].bitcast(FP8X4), lhsT_scale=w2_q[mt][1][:],
                                     rhs=own_words[h][:].bitcast(FP8X4), rhs_scale=own_plane[:, cols], start=True, stop=True)
                 res = keep.tile([P, HALF], F32, name="res%d_%d" % (mt, h))
-                nc.vector.tensor_tensor(res[:], e[:], gates[mt][:, cols], MULT)
-                queue = nc.sync if h == 0 else nc.scalar
-                queue.dma_start(out[mt * M_TILE : (mt + 1) * M_TILE, cols], res[:])
+                nc.vector.tensor_tensor(res[:], e[:], gate[:, h, mt, :], MULT)
+                nc.sync.dma_start(out[mt * M_TILE : (mt + 1) * M_TILE, cols], res[:])

@@ -14,11 +14,13 @@ U8 = mybir.dt.uint8
 FP8X4 = mybir.dt.float8_e4m3fn_x4
 SILU = mybir.ActivationFunctionType.Silu
 MULT = mybir.AluOpType.mult
+ADD = mybir.AluOpType.add
 
 P = 128
 PACK = 4
 M_TILE = 128
 HALF = S // 2
+WARM_PASSES = 12
 
 
 def tile_picked_phmix_silu_p_kernel(tc, x_words, x_scales, w1, w2, offs, own, out):
@@ -33,25 +35,23 @@ def tile_picked_phmix_silu_p_kernel(tc, x_words, x_scales, w1, w2, offs, own, ou
         own_sb = keep.tile([P, S // 16], U16, name="own_sb")
         scale_table = keep.tile([P, T], U8, name="scale_table", align_bytes=64)
         word_table = keep.tile([P, T], U32, name="word_table", align_bytes=64)
-        w1_raw = reuse.tile([P, PACK, N], F32, name="w1_raw", offset=8192, align_bytes=64)
-        w2_raw = [keep.tile([P, PACK, M_TILE], F32, name="w2_raw0"),
-                  reuse.tile([P, PACK, M_TILE], F32, name="w2_raw1", offset=0, align_bytes=64)]
+        w1_raw = keep.tile([P, PACK, N], F32, name="w1_raw")
+        w2_raw = reuse.tile([P, PACK, N], F32, name="w2_raw", offset=0, align_bytes=64)
         nc.sync.dma_start(offs_sb[:], offs)
         nc.sync.dma_start(scale_table[:].bitcast(I32), x_scales[0].bitcast(I32).unsqueeze(1).broadcast_to([16, 8, T // 4]))
         nc.sync.dma_start(own_sb[:], own)
-        nc.sync.dma_start(w1_raw[:], w1.rearrange("(p j) n -> p j n", j=PACK))
         nc.sync.dma_start(word_table[:].bitcast(I32), x_words[0].rearrange("p c r -> p (c r)").bitcast(I32))
-        w2_rows = w2.rearrange("(p j) n -> p j n", j=PACK)
-        for mt in range(m_tiles):
-            nc.sync.dma_start(w2_raw[mt][:], w2_rows[:, :, mt * M_TILE : (mt + 1) * M_TILE])
+        nc.sync.dma_start(w1_raw[:], w1.rearrange("(p j) n -> p j n", j=PACK))
+        nc.sync.dma_start(w2_raw[:], w2.rearrange("(p j) n -> p j n", j=PACK))
 
         warm = keep.tile([P, 8], F32, name="warm")
         nc.vector.memset(warm[:, 0:1], 0.0)
         nc.scalar.activation(warm[:, 1:2], warm[:, 0:1], SILU)
 
-        def cast(name, raw):
-            grouped = keep.tile([P, raw.shape[2], PACK], BF16, name=name, align_bytes=64)
-            nc.scalar.copy(grouped[:].rearrange("p (c i) t -> p c t i", i=4), raw[:].rearrange("p t (c i) -> p c t i", i=4))
+        def cast(name, raw, first, width, offset):
+            grouped = reuse.tile([P, width, PACK], BF16, name=name, offset=offset, align_bytes=64)
+            nc.scalar.copy(grouped[:].rearrange("p (c i) t -> p c t i", i=4),
+                           raw[:, :, first : first + width].rearrange("p t (c i) -> p c t i", i=4))
             return grouped
 
         def quantise(name, grouped):
@@ -60,55 +60,45 @@ def tile_picked_phmix_silu_p_kernel(tc, x_words, x_scales, w1, w2, offs, own, ou
             nc.vector.quantize_mx(out=codes[:].bitcast(FP8X4), scales=plane[:], in_=grouped[:].rearrange("p c t -> p (c t)"))
             return codes, plane
 
-        def pick_bytes(name, offsets):
-            picked = keep.tile([P, S], U8, name=name, align_bytes=64)
-            nc.vector.tensor_copy(picked[:], scale_table[:].indirect(offsets[:]))
-            return picked
+        planes = keep.tile([P, 2 * S], U8, name="planes", align_bytes=64)
+        nc.gpsimd.memset(planes[:].bitcast(I32), 0)
+        picked = keep.tile([P, 2 * S], U8, name="picked", align_bytes=64)
+        nc.vector.tensor_copy(picked[:, 0:S], scale_table[:].indirect(offs_sb[:]))
+        nc.vector.tensor_copy(picked[:, S : 2 * S], scale_table[:].indirect(own_sb[:]))
+        for j in range(4):
+            nc.sync.dma_start(planes[:].bitcast(I32)[j:P:32, :], picked[:].bitcast(I32)[8 * j : P : 32, :])
 
-        def place_rows(plane, picked):
-            src_rows = picked[:].bitcast(I32)
-            dst_rows = plane[:].bitcast(I32)
-            nc.vector.tensor_copy(dst_rows, src_rows)
-            for j in range(1, 4):
-                nc.sync.dma_start(dst_rows[j:P:32, :], src_rows[8 * j : P : 32, :])
-
-        def pick_words(words, offsets, h):
-            nc.vector.tensor_copy(words[:], word_table[:].indirect(offsets[:, h * HALF // 16 : (h + 1) * HALF // 16]))
-
-        head_plane = keep.tile([P, S], U8, name="head_plane", align_bytes=64)
-        place_rows(head_plane, pick_bytes("head_bytes", offs_sb))
-        own_bytes = pick_bytes("own_bytes", own_sb)
-        w1_codes, w1_plane = quantise("w1", cast("w1_grouped", w1_raw))
-        own_plane = reuse.tile([P, S], U8, name="own_plane", offset=8192, align_bytes=64)
-        place_rows(own_plane, own_bytes)
-
-        head_words = [keep.tile([P, HALF], U32, name="head_words%d" % h, align_bytes=64) for h in range(2)]
+        head_words = keep.tile([P, S], U32, name="head_words", align_bytes=64)
         for h in range(2):
-            pick_words(head_words[h], offs_sb, h)
+            nc.vector.tensor_copy(head_words[:, h * HALF : (h + 1) * HALF], word_table[:].indirect(offs_sb[:, h * HALF // 16 : (h + 1) * HALF // 16]))
         own_words = [keep.tile([P, HALF], U32, name="own_words0", align_bytes=64)]
-        pick_words(own_words[0], own_sb, 0)
+        nc.vector.tensor_copy(own_words[0][:], word_table[:].indirect(own_sb[:, 0 : HALF // 16]))
 
-        w2_q = [quantise("w2_%d" % mt, cast("w2_grouped%d" % mt, w2_raw[mt])) for mt in range(m_tiles)]
+        e_banks = [psum.tile([P, HALF], F32, name="e%d" % i) for i in range(2 * m_tiles)]
+        for i in range(WARM_PASSES):
+            nc.tensor.matmul_mx(out=e_banks[-1][0:32, 0:128], lhsT=head_words[:, 0:32].bitcast(FP8X4), lhsT_scale=picked[:, 0:32],
+                                rhs=head_words[:, 0:128].bitcast(FP8X4), rhs_scale=picked[:, 0:128], start=True, stop=True)
 
-        own_words.append(reuse.tile([P, HALF], U32, name="own_words1", offset=0, align_bytes=64))
-        pick_words(own_words[1], own_sb, 1)
+        w1_q = [quantise("w1_%d" % mt, cast("w1_grouped%d" % mt, w1_raw, mt * M_TILE, M_TILE, 4096 + 1024 * mt)) for mt in range(m_tiles)]
+        own_words.append(reuse.tile([P, HALF], U32, name="own_words1", offset=5120, align_bytes=64))
+        nc.vector.tensor_copy(own_words[1][:], word_table[:].indirect(own_sb[:, HALF // 16 : S // 16]))
+        w2_q = [quantise("w2_%d" % mt, cast("w2_grouped%d" % mt, w2_raw, mt * M_TILE, M_TILE, 6144 + 1024 * mt)) for mt in range(m_tiles)]
 
-        gate = reuse.tile([P, 2, m_tiles, HALF], F32, name="gate", offset=HALF * 4, align_bytes=64)
-        for h in range(2):
-            cols = slice(h * HALF, (h + 1) * HALF)
-            for mt in range(m_tiles):
-                chans = slice(mt * M_TILE, (mt + 1) * M_TILE)
-                y = psum.tile([P, HALF], F32, name="y%d_%d" % (mt, h))
-                nc.tensor.matmul_mx(out=y[:], lhsT=w1_codes[:, chans].bitcast(FP8X4), lhsT_scale=w1_plane[:, chans],
-                                    rhs=head_words[h][:].bitcast(FP8X4), rhs_scale=head_plane[:, cols], start=True, stop=True)
-                nc.scalar.activation(gate[:, h, mt, :], y[:], SILU)
+        gate = reuse.tile([P, m_tiles, S], F32, name="gate", offset=0, align_bytes=64)
+        for mt in range(m_tiles):
+            y = psum.tile([P, S], F32, name="y%d" % mt)
+            nc.tensor.matmul_mx(out=y[:], lhsT=w1_q[mt][0][:].bitcast(FP8X4), lhsT_scale=w1_q[mt][1][:],
+                                rhs=head_words[:].bitcast(FP8X4), rhs_scale=planes[:, 0:S], start=True, stop=True)
+            for h in range(2):
+                cols = slice(h * HALF, (h + 1) * HALF)
+                nc.scalar.activation(gate[:, mt, cols], y[:, cols], SILU)
 
-        for h in range(2):
-            cols = slice(h * HALF, (h + 1) * HALF)
-            for mt in range(m_tiles):
-                e = psum.tile([P, HALF], F32, name="e%d_%d" % (mt, h))
+        for mt in range(m_tiles):
+            for h in range(2):
+                cols = slice(h * HALF, (h + 1) * HALF)
+                e = e_banks[2 * mt + h]
                 nc.tensor.matmul_mx(out=e[:], lhsT=w2_q[mt][0][:].bitcast(FP8X4), lhsT_scale=w2_q[mt][1][:],
-                                    rhs=own_words[h][:].bitcast(FP8X4), rhs_scale=own_plane[:, cols], start=True, stop=True)
+                                    rhs=own_words[h][:].bitcast(FP8X4), rhs_scale=planes[:, S + h * HALF : S + (h + 1) * HALF], start=True, stop=True)
                 res = keep.tile([P, HALF], F32, name="res%d_%d" % (mt, h))
-                nc.vector.tensor_tensor(res[:], e[:], gate[:, h, mt, :], MULT)
+                nc.vector.tensor_tensor(res[:], e[:], gate[:, mt, cols], MULT)
                 nc.sync.dma_start(out[mt * M_TILE : (mt + 1) * M_TILE, cols], res[:])

@@ -20,7 +20,8 @@ P = 128
 PACK = 4
 M_TILE = 128
 HALF = S // 2
-WARM_PASSES = 12
+WARM_PASSES = 14
+SCALAR_SHARE = 64
 
 
 def tile_picked_phmix_silu_p_kernel(tc, x_words, x_scales, w1, w2, offs, own, out):
@@ -48,16 +49,13 @@ def tile_picked_phmix_silu_p_kernel(tc, x_words, x_scales, w1, w2, offs, own, ou
         nc.vector.memset(warm[:, 0:1], 0.0)
         nc.scalar.activation(warm[:, 1:2], warm[:, 0:1], SILU)
 
-        def cast(name, raw, first, width, offset):
-            grouped = reuse.tile([P, width, PACK], BF16, name=name, offset=offset, align_bytes=64)
-            nc.scalar.copy(grouped[:].rearrange("p (c i) t -> p c t i", i=4),
-                           raw[:, :, first : first + width].rearrange("p t (c i) -> p c t i", i=4))
-            return grouped
+        def cast(copy, grouped, raw):
+            copy(grouped.rearrange("p (c i) t -> p c t i", i=4), raw.rearrange("p t (c i) -> p c t i", i=4))
 
         def quantise(name, grouped):
             codes = keep.tile([P, grouped.shape[1]], U32, name=name + "_codes", align_bytes=64)
             plane = keep.tile([P, grouped.shape[1]], U8, name=name + "_plane", align_bytes=64)
-            nc.vector.quantize_mx(out=codes[:].bitcast(FP8X4), scales=plane[:], in_=grouped[:].rearrange("p c t -> p (c t)"))
+            nc.vector.quantize_mx(out=codes[:].bitcast(FP8X4), scales=plane[:], in_=grouped.rearrange("p c t -> p (c t)"))
             return codes, plane
 
         planes = keep.tile([P, 2 * S], U8, name="planes", align_bytes=64)
@@ -66,39 +64,49 @@ def tile_picked_phmix_silu_p_kernel(tc, x_words, x_scales, w1, w2, offs, own, ou
         nc.vector.tensor_copy(picked[:, 0:S], scale_table[:].indirect(offs_sb[:]))
         nc.vector.tensor_copy(picked[:, S : 2 * S], scale_table[:].indirect(own_sb[:]))
         for j in range(4):
-            nc.sync.dma_start(planes[:].bitcast(I32)[j:P:32, :], picked[:].bitcast(I32)[8 * j : P : 32, :])
+            queue = nc.sync if j % 2 == 0 else nc.scalar
+            queue.dma_start(planes[:].bitcast(I32)[j:P:32, :], picked[:].bitcast(I32)[8 * j : P : 32, :])
 
         head_words = keep.tile([P, S], U32, name="head_words", align_bytes=64)
         for h in range(2):
             nc.vector.tensor_copy(head_words[:, h * HALF : (h + 1) * HALF], word_table[:].indirect(offs_sb[:, h * HALF // 16 : (h + 1) * HALF // 16]))
-        own_words = [keep.tile([P, HALF], U32, name="own_words0", align_bytes=64)]
-        nc.vector.tensor_copy(own_words[0][:], word_table[:].indirect(own_sb[:, 0 : HALF // 16]))
+        own_words = keep.tile([P, S], U32, name="own_words", align_bytes=64)
+        nc.vector.tensor_copy(own_words[:], word_table[:].indirect(own_sb[:]))
 
         e_banks = [psum.tile([P, HALF], F32, name="e%d" % i) for i in range(2 * m_tiles)]
         for i in range(WARM_PASSES):
             nc.tensor.matmul_mx(out=e_banks[-1][0:32, 0:128], lhsT=head_words[:, 0:32].bitcast(FP8X4), lhsT_scale=picked[:, 0:32],
                                 rhs=head_words[:, 0:128].bitcast(FP8X4), rhs_scale=picked[:, 0:128], start=True, stop=True)
 
-        w1_q = [quantise("w1_%d" % mt, cast("w1_grouped%d" % mt, w1_raw, mt * M_TILE, M_TILE, 4096 + 1024 * mt)) for mt in range(m_tiles)]
-        own_words.append(reuse.tile([P, HALF], U32, name="own_words1", offset=5120, align_bytes=64))
-        nc.vector.tensor_copy(own_words[1][:], word_table[:].indirect(own_sb[:, HALF // 16 : S // 16]))
-        w2_q = [quantise("w2_%d" % mt, cast("w2_grouped%d" % mt, w2_raw, mt * M_TILE, M_TILE, 6144 + 1024 * mt)) for mt in range(m_tiles)]
+        w1_grouped = keep.tile([P, N, PACK], BF16, name="w1_grouped", align_bytes=64)
+        w1_q = []
+        for mt in range(m_tiles):
+            chans = slice(mt * M_TILE, (mt + 1) * M_TILE)
+            cast(nc.scalar.copy, w1_grouped[:, chans, :], w1_raw[:, :, chans])
+            w1_q.append(quantise("w1_%d" % mt, w1_grouped[:, chans, :]))
+
+        w2_grouped = [reuse.tile([P, M_TILE, PACK], BF16, name="w2_grouped%d" % mt, offset=4096 + 1024 * mt, align_bytes=64) for mt in range(m_tiles)]
+        cast(nc.scalar.copy, w2_grouped[0][:], w2_raw[:, :, 0:M_TILE])
+        cast(nc.scalar.copy, w2_grouped[1][:, 0:SCALAR_SHARE, :], w2_raw[:, :, M_TILE : M_TILE + SCALAR_SHARE])
+        cast(nc.vector.tensor_copy, w2_grouped[1][:, SCALAR_SHARE:M_TILE, :], w2_raw[:, :, M_TILE + SCALAR_SHARE : N])
+        w2_q = [quantise("w2_0", w2_grouped[0][:])]
+        w2_q.append(quantise("w2_1", w2_grouped[1][:]))
 
         gate = reuse.tile([P, m_tiles, S], F32, name="gate", offset=0, align_bytes=64)
         for mt in range(m_tiles):
-            y = psum.tile([P, S], F32, name="y%d" % mt)
-            nc.tensor.matmul_mx(out=y[:], lhsT=w1_q[mt][0][:].bitcast(FP8X4), lhsT_scale=w1_q[mt][1][:],
-                                rhs=head_words[:].bitcast(FP8X4), rhs_scale=planes[:, 0:S], start=True, stop=True)
             for h in range(2):
                 cols = slice(h * HALF, (h + 1) * HALF)
-                nc.scalar.activation(gate[:, mt, cols], y[:, cols], SILU)
+                y = psum.tile([P, HALF], F32, name="y%d_%d" % (mt, h))
+                nc.tensor.matmul_mx(out=y[:], lhsT=w1_q[mt][0][:].bitcast(FP8X4), lhsT_scale=w1_q[mt][1][:],
+                                    rhs=head_words[:, cols].bitcast(FP8X4), rhs_scale=planes[:, cols], start=True, stop=True)
+                nc.scalar.activation(gate[:, mt, cols], y[:], SILU)
 
         for mt in range(m_tiles):
             for h in range(2):
                 cols = slice(h * HALF, (h + 1) * HALF)
                 e = e_banks[2 * mt + h]
                 nc.tensor.matmul_mx(out=e[:], lhsT=w2_q[mt][0][:].bitcast(FP8X4), lhsT_scale=w2_q[mt][1][:],
-                                    rhs=own_words[h][:].bitcast(FP8X4), rhs_scale=planes[:, S + h * HALF : S + (h + 1) * HALF], start=True, stop=True)
+                                    rhs=own_words[:, cols].bitcast(FP8X4), rhs_scale=planes[:, S + h * HALF : S + (h + 1) * HALF], start=True, stop=True)
                 res = keep.tile([P, HALF], F32, name="res%d_%d" % (mt, h))
                 nc.vector.tensor_tensor(res[:], e[:], gate[:, mt, cols], MULT)
                 nc.sync.dma_start(out[mt * M_TILE : (mt + 1) * M_TILE, cols], res[:])

@@ -39,8 +39,10 @@ def tile_picked_phmix_silu_p_kernel(tc, x_words, x_scales, w1, w2, offs, own, ou
         w1_raw = keep.tile([P, PACK, N], F32, name="w1_raw")
         w2_raw = reuse.tile([P, PACK, N], F32, name="w2_raw", offset=0, align_bytes=64)
         nc.sync.dma_start(offs_sb[:], offs)
-        nc.sync.dma_start(scale_table[:].bitcast(I32), x_scales[0].bitcast(I32).unsqueeze(1).broadcast_to([16, 8, T // 4]))
         nc.sync.dma_start(own_sb[:], own)
+        table_rows = scale_table[:].bitcast(I32)
+        nc.vector.memset(table_rows, 0)
+        nc.sync.dma_start(table_rows[0:P:8, :], x_scales[0].bitcast(I32))
         nc.sync.dma_start(word_table[:].bitcast(I32), x_words[0].rearrange("p c r -> p (c r)").bitcast(I32))
         nc.sync.dma_start(w1_raw[:], w1.rearrange("(p j) n -> p j n", j=PACK))
         nc.sync.dma_start(w2_raw[:], w2.rearrange("(p j) n -> p j n", j=PACK))

@@ -22,6 +22,7 @@ M_TILE = 128
 HALF = S // 2
 WARM_PASSES = 14
 SCALAR_SHARE = 64
+FIRST_WORDS = 256
 
 
 def tile_picked_phmix_silu_p_kernel(tc, x_words, x_scales, w1, w2, offs, own, out):
@@ -40,10 +41,12 @@ def tile_picked_phmix_silu_p_kernel(tc, x_words, x_scales, w1, w2, offs, own, ou
         w2_raw = reuse.tile([P, PACK, N], F32, name="w2_raw", offset=0, align_bytes=64)
         nc.sync.dma_start(offs_sb[:], offs)
         nc.sync.dma_start(own_sb[:], own)
+        word_rows = x_words[0].rearrange("p c r -> p (c r)").bitcast(I32)
+        nc.sync.dma_start(word_table[:, 0:FIRST_WORDS].bitcast(I32), word_rows[:, 0:FIRST_WORDS])
         table_rows = scale_table[:].bitcast(I32)
         nc.vector.memset(table_rows, 0)
         nc.sync.dma_start(table_rows[0:P:8, :], x_scales[0].bitcast(I32))
-        nc.sync.dma_start(word_table[:].bitcast(I32), x_words[0].rearrange("p c r -> p (c r)").bitcast(I32))
+        nc.sync.dma_start(word_table[:, FIRST_WORDS:T].bitcast(I32), word_rows[:, FIRST_WORDS:T])
         nc.sync.dma_start(w1_raw[:], w1.rearrange("(p j) n -> p j n", j=PACK))
         nc.sync.dma_start(w2_raw[:], w2.rearrange("(p j) n -> p j n", j=PACK))
 
@@ -53,6 +56,9 @@ def tile_picked_phmix_silu_p_kernel(tc, x_words, x_scales, w1, w2, offs, own, ou
 
         def cast(copy, grouped, raw):
             copy(grouped.rearrange("p (c i) t -> p c t i", i=4), raw.rearrange("p t (c i) -> p c t i", i=4))
+
+        def gpsimd_copy(dst, src):
+            nc.gpsimd.tensor_scalar(dst, src, 1.0, 0.0, MULT, ADD)
 
         def quantise(name, grouped):
             codes = keep.tile([P, grouped.shape[1]], U32, name=name + "_codes", align_bytes=64)
@@ -90,7 +96,7 @@ def tile_picked_phmix_silu_p_kernel(tc, x_words, x_scales, w1, w2, offs, own, ou
         w2_grouped = [reuse.tile([P, M_TILE, PACK], BF16, name="w2_grouped%d" % mt, offset=4096 + 1024 * mt, align_bytes=64) for mt in range(m_tiles)]
         cast(nc.scalar.copy, w2_grouped[0][:], w2_raw[:, :, 0:M_TILE])
         cast(nc.scalar.copy, w2_grouped[1][:, 0:SCALAR_SHARE, :], w2_raw[:, :, M_TILE : M_TILE + SCALAR_SHARE])
-        cast(nc.vector.tensor_copy, w2_grouped[1][:, SCALAR_SHARE:M_TILE, :], w2_raw[:, :, M_TILE + SCALAR_SHARE : N])
+        cast(gpsimd_copy, w2_grouped[1][:, SCALAR_SHARE:M_TILE, :], w2_raw[:, :, M_TILE + SCALAR_SHARE : N])
         w2_q = [quantise("w2_0", w2_grouped[0][:])]
         w2_q.append(quantise("w2_1", w2_grouped[1][:]))
 

@@ -20,7 +20,7 @@ P = 128
 PACK = 4
 M_TILE = 128
 HALF = S // 2
-WARM_PASSES = 14
+WARM_PASSES = 13
 SCALAR_SHARE = 64
 FIRST_WORDS = 256
 
@@ -37,7 +37,7 @@ def tile_picked_phmix_silu_p_kernel(tc, x_words, x_scales, w1, w2, offs, own, ou
         own_sb = keep.tile([P, S // 16], U16, name="own_sb")
         scale_table = keep.tile([P, T], U8, name="scale_table", align_bytes=64)
         word_table = keep.tile([P, T], U32, name="word_table", align_bytes=64)
-        w1_raw = keep.tile([P, PACK, N], F32, name="w1_raw")
+        w1_raw = reuse.tile([P, PACK, N], F32, name="w1_raw", offset=8192, align_bytes=64)
         w2_raw = reuse.tile([P, PACK, N], F32, name="w2_raw", offset=0, align_bytes=64)
         nc.sync.dma_start(offs_sb[:], offs)
         nc.sync.dma_start(own_sb[:], own)
@@ -78,8 +78,8 @@ def tile_picked_phmix_silu_p_kernel(tc, x_words, x_scales, w1, w2, offs, own, ou
         head_words = keep.tile([P, S], U32, name="head_words", align_bytes=64)
         for h in range(2):
             nc.vector.tensor_copy(head_words[:, h * HALF : (h + 1) * HALF], word_table[:].indirect(offs_sb[:, h * HALF // 16 : (h + 1) * HALF // 16]))
-        own_words = keep.tile([P, S], U32, name="own_words", align_bytes=64)
-        nc.vector.tensor_copy(own_words[:], word_table[:].indirect(own_sb[:]))
+        own_words = [keep.tile([P, HALF], U32, name="own_words0", align_bytes=64)]
+        nc.vector.tensor_copy(own_words[0][:], word_table[:].indirect(own_sb[:, 0 : HALF // 16]))
 
         e_banks = [psum.tile([P, HALF], F32, name="e%d" % i) for i in range(2 * m_tiles)]
         for i in range(WARM_PASSES):
@@ -87,11 +87,12 @@ def tile_picked_phmix_silu_p_kernel(tc, x_words, x_scales, w1, w2, offs, own, ou
                                 rhs=head_words[:, 0:128].bitcast(FP8X4), rhs_scale=picked[:, 0:128], start=True, stop=True)
 
         w1_grouped = keep.tile([P, N, PACK], BF16, name="w1_grouped", align_bytes=64)
-        w1_q = []
-        for mt in range(m_tiles):
-            chans = slice(mt * M_TILE, (mt + 1) * M_TILE)
-            cast(nc.scalar.copy, w1_grouped[:, chans, :], w1_raw[:, :, chans])
-            w1_q.append(quantise("w1_%d" % mt, w1_grouped[:, chans, :]))
+        cast(nc.scalar.copy, w1_grouped[:, 0:M_TILE, :], w1_raw[:, :, 0:M_TILE])
+        cast(nc.scalar.copy, w1_grouped[:, M_TILE : M_TILE + SCALAR_SHARE, :], w1_raw[:, :, M_TILE : M_TILE + SCALAR_SHARE])
+        cast(gpsimd_copy, w1_grouped[:, M_TILE + SCALAR_SHARE : N, :], w1_raw[:, :, M_TILE + SCALAR_SHARE : N])
+        w1_q = [quantise("w1_%d" % mt, w1_grouped[:, mt * M_TILE : (mt + 1) * M_TILE, :]) for mt in range(m_tiles)]
+        own_words.append(reuse.tile([P, HALF], U32, name="own_words1", offset=8192, align_bytes=64))
+        nc.vector.tensor_copy(own_words[1][:], word_table[:].indirect(own_sb[:, HALF // 16 : S // 16]))
 
         w2_grouped = [reuse.tile([P, M_TILE, PACK], BF16, name="w2_grouped%d" % mt, offset=4096 + 1024 * mt, align_bytes=64) for mt in range(m_tiles)]
         cast(nc.scalar.copy, w2_grouped[0][:], w2_raw[:, :, 0:M_TILE])
@@ -114,7 +115,7 @@ def tile_picked_phmix_silu_p_kernel(tc, x_words, x_scales, w1, w2, offs, own, ou
                 cols = slice(h * HALF, (h + 1) * HALF)
                 e = e_banks[2 * mt + h]
                 nc.tensor.matmul_mx(out=e[:], lhsT=w2_q[mt][0][:].bitcast(FP8X4), lhsT_scale=w2_q[mt][1][:],
-                                    rhs=own_words[:, cols].bitcast(FP8X4), rhs_scale=planes[:, S + h * HALF : S + (h + 1) * HALF], start=True, stop=True)
+                                    rhs=own_words[h][:].bitcast(FP8X4), rhs_scale=planes[:, S + h * HALF : S + (h + 1) * HALF], start=True, stop=True)
                 res = keep.tile([P, HALF], F32, name="res%d_%d" % (mt, h))
                 nc.vector.tensor_tensor(res[:], e[:], gate[:, mt, cols], MULT)
                 nc.sync.dma_start(out[mt * M_TILE : (mt + 1) * M_TILE, cols], res[:])

@@ -20,9 +20,8 @@ P = 128
 PACK = 4
 M_TILE = 128
 HALF = S // 2
-WARM_PASSES = 13
 SCALAR_SHARE = 64
-FIRST_WORDS = 256
+FIRST_WORDS = 448
 
 
 def tile_picked_phmix_silu_p_kernel(tc, x_words, x_scales, w1, w2, offs, own, out):
@@ -37,12 +36,12 @@ def tile_picked_phmix_silu_p_kernel(tc, x_words, x_scales, w1, w2, offs, own, ou
         own_sb = keep.tile([P, S // 16], U16, name="own_sb")
         scale_table = keep.tile([P, T], U8, name="scale_table", align_bytes=64)
         word_table = keep.tile([P, T], U32, name="word_table", align_bytes=64)
-        w1_raw = reuse.tile([P, PACK, N], F32, name="w1_raw", offset=8192, align_bytes=64)
-        w2_raw = reuse.tile([P, PACK, N], F32, name="w2_raw", offset=0, align_bytes=64)
-        nc.sync.dma_start(offs_sb[:], offs)
-        nc.sync.dma_start(own_sb[:], own)
+        w1_raw = reuse.tile([P, PACK, N], F32, name="w1_raw", offset=12288, align_bytes=64)
+        w2_raw = reuse.tile([P, PACK, N], F32, name="w2_raw", offset=4096, align_bytes=64)
         word_rows = x_words[0].rearrange("p c r -> p (c r)").bitcast(I32)
         nc.sync.dma_start(word_table[:, 0:FIRST_WORDS].bitcast(I32), word_rows[:, 0:FIRST_WORDS])
+        nc.sync.dma_start(offs_sb[:], offs)
+        nc.sync.dma_start(own_sb[:], own)
         table_rows = scale_table[:].bitcast(I32)
         nc.vector.memset(table_rows, 0)
         nc.sync.dma_start(table_rows[0:P:8, :], x_scales[0].bitcast(I32))
@@ -66,56 +65,57 @@ def tile_picked_phmix_silu_p_kernel(tc, x_words, x_scales, w1, w2, offs, own, ou
             nc.vector.quantize_mx(out=codes[:].bitcast(FP8X4), scales=plane[:], in_=grouped.rearrange("p c t -> p (c t)"))
             return codes, plane
 
-        planes = keep.tile([P, 2 * S], U8, name="planes", align_bytes=64)
-        nc.gpsimd.memset(planes[:].bitcast(I32), 0)
-        picked = keep.tile([P, 2 * S], U8, name="picked", align_bytes=64)
-        nc.vector.tensor_copy(picked[:, 0:S], scale_table[:].indirect(offs_sb[:]))
-        nc.vector.tensor_copy(picked[:, S : 2 * S], scale_table[:].indirect(own_sb[:]))
+        head_plane = keep.tile([P, S], U8, name="head_plane", align_bytes=64)
+        nc.gpsimd.memset(head_plane[:].bitcast(I32), 0)
+        head_picked = keep.tile([P, S], U8, name="head_picked", align_bytes=64)
+        nc.vector.tensor_copy(head_picked[:], scale_table[:].indirect(offs_sb[:]))
         for j in range(4):
-            queue = nc.sync if j % 2 == 0 else nc.scalar
-            queue.dma_start(planes[:].bitcast(I32)[j:P:32, :], picked[:].bitcast(I32)[8 * j : P : 32, :])
+            nc.scalar.dma_start(head_plane[:].bitcast(I32)[j:P:32, :], head_picked[:].bitcast(I32)[8 * j : P : 32, :])
+        own_picked = keep.tile([P, S], U8, name="own_picked", align_bytes=64)
+        nc.vector.tensor_copy(own_picked[:], scale_table[:].indirect(own_sb[:]))
+        own_plane = keep.tile([P, S], U8, name="own_plane", align_bytes=64)
+        nc.vector.tensor_copy(own_plane[:].bitcast(I32), own_picked[:].bitcast(I32))
+        for j in range(1, 4):
+            nc.sync.dma_start(own_plane[:].bitcast(I32)[j:P:32, :], own_picked[:].bitcast(I32)[8 * j : P : 32, :])
 
         head_words = keep.tile([P, S], U32, name="head_words", align_bytes=64)
-        for h in range(2):
-            nc.vector.tensor_copy(head_words[:, h * HALF : (h + 1) * HALF], word_table[:].indirect(offs_sb[:, h * HALF // 16 : (h + 1) * HALF // 16]))
-        own_words = [keep.tile([P, HALF], U32, name="own_words0", align_bytes=64)]
-        nc.vector.tensor_copy(own_words[0][:], word_table[:].indirect(own_sb[:, 0 : HALF // 16]))
+        nc.vector.tensor_copy(head_words[:], word_table[:].indirect(offs_sb[:]))
 
         e_banks = [psum.tile([P, HALF], F32, name="e%d" % i) for i in range(2 * m_tiles)]
-        for i in range(WARM_PASSES):
-            nc.tensor.matmul_mx(out=e_banks[-1][0:32, 0:128], lhsT=head_words[:, 0:32].bitcast(FP8X4), lhsT_scale=picked[:, 0:32],
-                                rhs=head_words[:, 0:128].bitcast(FP8X4), rhs_scale=picked[:, 0:128], start=True, stop=True)
 
         w1_grouped = keep.tile([P, N, PACK], BF16, name="w1_grouped", align_bytes=64)
         cast(nc.scalar.copy, w1_grouped[:, 0:M_TILE, :], w1_raw[:, :, 0:M_TILE])
         cast(nc.scalar.copy, w1_grouped[:, M_TILE : M_TILE + SCALAR_SHARE, :], w1_raw[:, :, M_TILE : M_TILE + SCALAR_SHARE])
         cast(gpsimd_copy, w1_grouped[:, M_TILE + SCALAR_SHARE : N, :], w1_raw[:, :, M_TILE + SCALAR_SHARE : N])
-        w1_q = [quantise("w1_%d" % mt, w1_grouped[:, mt * M_TILE : (mt + 1) * M_TILE, :]) for mt in range(m_tiles)]
-        own_words.append(reuse.tile([P, HALF], U32, name="own_words1", offset=8192, align_bytes=64))
-        nc.vector.tensor_copy(own_words[1][:], word_table[:].indirect(own_sb[:, HALF // 16 : S // 16]))
+        w1_q = [quantise("w1_0", w1_grouped[:, 0:M_TILE, :])]
+        w1_q.append(quantise("w1_1", w1_grouped[:, M_TILE:N, :]))
+        own_words = [reuse.tile([P, HALF], U32, name="own_words0", offset=12288, align_bytes=64)]
+        nc.vector.tensor_copy(own_words[0][:], word_table[:].indirect(own_sb[:, 0 : HALF // 16]))
 
-        w2_grouped = [reuse.tile([P, M_TILE, PACK], BF16, name="w2_grouped%d" % mt, offset=4096 + 1024 * mt, align_bytes=64) for mt in range(m_tiles)]
+        w2_grouped = [reuse.tile([P, M_TILE, PACK], BF16, name="w2_grouped%d" % mt, offset=8192 + 1024 * mt, align_bytes=64) for mt in range(m_tiles)]
         cast(nc.scalar.copy, w2_grouped[0][:], w2_raw[:, :, 0:M_TILE])
         cast(nc.scalar.copy, w2_grouped[1][:, 0:SCALAR_SHARE, :], w2_raw[:, :, M_TILE : M_TILE + SCALAR_SHARE])
         cast(gpsimd_copy, w2_grouped[1][:, SCALAR_SHARE:M_TILE, :], w2_raw[:, :, M_TILE + SCALAR_SHARE : N])
         w2_q = [quantise("w2_0", w2_grouped[0][:])]
         w2_q.append(quantise("w2_1", w2_grouped[1][:]))
+        own_words.append(reuse.tile([P, HALF], U32, name="own_words1", offset=6144, align_bytes=64))
+        nc.vector.tensor_copy(own_words[1][:], word_table[:].indirect(own_sb[:, HALF // 16 : S // 16]))
 
-        gate = reuse.tile([P, m_tiles, S], F32, name="gate", offset=0, align_bytes=64)
-        for mt in range(m_tiles):
-            for h in range(2):
+        gate = reuse.tile([P, m_tiles, S], F32, name="gate", offset=1024, align_bytes=64)
+        for h in range(2):
+            for mt in range(m_tiles):
                 cols = slice(h * HALF, (h + 1) * HALF)
                 y = psum.tile([P, HALF], F32, name="y%d_%d" % (mt, h))
                 nc.tensor.matmul_mx(out=y[:], lhsT=w1_q[mt][0][:].bitcast(FP8X4), lhsT_scale=w1_q[mt][1][:],
-                                    rhs=head_words[:, cols].bitcast(FP8X4), rhs_scale=planes[:, cols], start=True, stop=True)
+                                    rhs=head_words[:, cols].bitcast(FP8X4), rhs_scale=head_plane[:, cols], start=True, stop=True)
                 nc.scalar.activation(gate[:, mt, cols], y[:], SILU)
 
-        for mt in range(m_tiles):
-            for h in range(2):
+        for h in range(2):
+            for mt in range(m_tiles):
                 cols = slice(h * HALF, (h + 1) * HALF)
                 e = e_banks[2 * mt + h]
                 nc.tensor.matmul_mx(out=e[:], lhsT=w2_q[mt][0][:].bitcast(FP8X4), lhsT_scale=w2_q[mt][1][:],
-                                    rhs=own_words[h][:].bitcast(FP8X4), rhs_scale=planes[:, S + h * HALF : S + (h + 1) * HALF], start=True, stop=True)
+                                    rhs=own_words[h][:].bitcast(FP8X4), rhs_scale=own_plane[:, cols], start=True, stop=True)
                 res = keep.tile([P, HALF], F32, name="res%d_%d" % (mt, h))
                 nc.vector.tensor_tensor(res[:], e[:], gate[:, mt, cols], MULT)
                 nc.sync.dma_start(out[mt * M_TILE : (mt + 1) * M_TILE, cols], res[:])

@@ -20,7 +20,7 @@ P = 128
 PACK = 4
 M_TILE = 128
 HALF = S // 2
-SCALAR_SHARE = 64
+SCALAR_SHARE = 48
 FIRST_WORDS = 448
 
 
@@ -66,7 +66,7 @@ def tile_picked_phmix_silu_p_kernel(tc, x_words, x_scales, w1, w2, offs, own, ou
             return codes, plane
 
         head_plane = keep.tile([P, S], U8, name="head_plane", align_bytes=64)
-        nc.gpsimd.memset(head_plane[:].bitcast(I32), 0)
+        nc.vector.memset(head_plane[:].bitcast(I32), 0)
         head_picked = keep.tile([P, S], U8, name="head_picked", align_bytes=64)
         nc.vector.tensor_copy(head_picked[:], scale_table[:].indirect(offs_sb[:]))
         for j in range(4):
@@ -101,7 +101,7 @@ def tile_picked_phmix_silu_p_kernel(tc, x_words, x_scales, w1, w2, offs, own, ou
         own_words.append(reuse.tile([P, HALF], U32, name="own_words1", offset=6144, align_bytes=64))
         nc.vector.tensor_copy(own_words[1][:], word_table[:].indirect(own_sb[:, HALF // 16 : S // 16]))
 
-        gate = reuse.tile([P, m_tiles, S], F32, name="gate", offset=1024, align_bytes=64)
+        gate = keep.tile([P, m_tiles, S], F32, name="gate", align_bytes=64)
         for h in range(2):
             for mt in range(m_tiles):
                 cols = slice(h * HALF, (h + 1) * HALF)

@@ -22,6 +22,8 @@ M_TILE = 128
 HALF = S // 2
 SCALAR_SHARE = 48
 FIRST_WORDS = 448
+TABLE_ROW = 4
+OWN_ROW = 8
 
 
 def tile_picked_phmix_silu_p_kernel(tc, x_words, x_scales, w1, w2, offs, own, out):
@@ -44,7 +46,7 @@ def tile_picked_phmix_silu_p_kernel(tc, x_words, x_scales, w1, w2, offs, own, ou
         nc.sync.dma_start(own_sb[:], own)
         table_rows = scale_table[:].bitcast(I32)
         nc.vector.memset(table_rows, 0)
-        nc.sync.dma_start(table_rows[0:P:8, :], x_scales[0].bitcast(I32))
+        nc.sync.dma_start(table_rows[TABLE_ROW:P:8, :], x_scales[0].bitcast(I32))
         nc.sync.dma_start(word_table[:, FIRST_WORDS:T].bitcast(I32), word_rows[:, FIRST_WORDS:T])
         nc.sync.dma_start(w1_raw[:], w1.rearrange("(p j) n -> p j n", j=PACK))
         nc.sync.dma_start(w2_raw[:], w2.rearrange("(p j) n -> p j n", j=PACK))
@@ -70,13 +72,13 @@ def tile_picked_phmix_silu_p_kernel(tc, x_words, x_scales, w1, w2, offs, own, ou
         head_picked = keep.tile([P, S], U8, name="head_picked", align_bytes=64)
         nc.vector.tensor_copy(head_picked[:], scale_table[:].indirect(offs_sb[:]))
         for j in range(4):
-            nc.scalar.dma_start(head_plane[:].bitcast(I32)[j:P:32, :], head_picked[:].bitcast(I32)[8 * j : P : 32, :])
+            nc.scalar.dma_start(head_plane[:].bitcast(I32)[j:P:32, :], head_picked[:].bitcast(I32)[TABLE_ROW + 8 * j : P : 32, :])
         own_picked = keep.tile([P, S], U8, name="own_picked", align_bytes=64)
         nc.vector.tensor_copy(own_picked[:], scale_table[:].indirect(own_sb[:]))
         own_plane = keep.tile([P, S], U8, name="own_plane", align_bytes=64)
-        nc.vector.tensor_copy(own_plane[:].bitcast(I32), own_picked[:].bitcast(I32))
-        for j in range(1, 4):
-            nc.sync.dma_start(own_plane[:].bitcast(I32)[j:P:32, :], own_picked[:].bitcast(I32)[8 * j : P : 32, :])
+        nc.vector.memset(own_plane[:].bitcast(I32), 0)
+        for j in range(4):
+            nc.sync.dma_start(own_plane[:].bitcast(I32)[OWN_ROW + j : P : 32, :], own_picked[:].bitcast(I32)[TABLE_ROW + 8 * j : P : 32, :])
 
         head_words = keep.tile([P, S], U32, name="head_words", align_bytes=64)
         nc.vector.tensor_copy(head_words[:], word_table[:].indirect(offs_sb[:]))
@@ -115,7 +117,7 @@ def tile_picked_phmix_silu_p_kernel(tc, x_words, x_scales, w1, w2, offs, own, ou
                 cols = slice(h * HALF, (h + 1) * HALF)
                 e = e_banks[2 * mt + h]
                 nc.tensor.matmul_mx(out=e[:], lhsT=w2_q[mt][0][:].bitcast(FP8X4), lhsT_scale=w2_q[mt][1][:],
-                                    rhs=own_words[h][:].bitcast(FP8X4), rhs_scale=own_plane[:, cols], start=True, stop=True)
+                                    rhs=own_words[h][:].bitcast(FP8X4), rhs_scale=own_plane[OWN_ROW:P, cols], start=True, stop=True)
                 res = keep.tile([P, HALF], F32, name="res%d_%d" % (mt, h))
                 nc.vector.tensor_tensor(res[:], e[:], gate[:, mt, cols], MULT)
                 nc.sync.dma_start(out[mt * M_TILE : (mt + 1) * M_TILE, cols], res[:])

@@ -24,6 +24,7 @@ SCALAR_SHARE = 48
 FIRST_WORDS = 448
 TABLE_ROW = 4
 OWN_ROW = 8
+PIECE = 128
 
 
 def tile_picked_phmix_silu_p_kernel(tc, x_words, x_scales, w1, w2, offs, own, out):
@@ -67,23 +68,28 @@ def tile_picked_phmix_silu_p_kernel(tc, x_words, x_scales, w1, w2, offs, own, ou
             nc.vector.quantize_mx(out=codes[:].bitcast(FP8X4), scales=plane[:], in_=grouped.rearrange("p c t -> p (c t)"))
             return codes, plane
 
-        head_plane = keep.tile([P, S], U8, name="head_plane", align_bytes=64)
-        nc.vector.memset(head_plane[:].bitcast(I32), 0)
-        head_picked = keep.tile([P, S], U8, name="head_picked", align_bytes=64)
-        nc.vector.tensor_copy(head_picked[:], scale_table[:].indirect(offs_sb[:]))
+        early_plane = keep.tile([P, S + HALF], U8, name="early_plane", align_bytes=64)
+        nc.vector.memset(early_plane[:].bitcast(I32), 0)
+        late_plane = keep.tile([P, HALF], U8, name="late_plane", align_bytes=64)
+        nc.vector.memset(late_plane[:].bitcast(I32), 0)
+        early_picked = keep.tile([P, S + HALF], U8, name="early_picked", align_bytes=64)
+        nc.vector.tensor_copy(early_picked[:, 0:S], scale_table[:].indirect(offs_sb[:]))
+        nc.vector.tensor_copy(early_picked[:, S : S + HALF], scale_table[:].indirect(own_sb[:, 0 : HALF // 16]))
         for j in range(4):
-            nc.scalar.dma_start(head_plane[:].bitcast(I32)[j:P:32, :], head_picked[:].bitcast(I32)[TABLE_ROW + 8 * j : P : 32, :])
-        own_picked = keep.tile([P, S], U8, name="own_picked", align_bytes=64)
-        nc.vector.tensor_copy(own_picked[:], scale_table[:].indirect(own_sb[:]))
-        own_plane = keep.tile([P, S], U8, name="own_plane", align_bytes=64)
-        nc.vector.memset(own_plane[:].bitcast(I32), 0)
+            nc.scalar.dma_start(early_plane[:].bitcast(I32)[j:P:32, :], early_picked[:].bitcast(I32)[TABLE_ROW + 8 * j : P : 32, :])
+        late_picked = keep.tile([P, HALF], U8, name="late_picked", align_bytes=64)
+        nc.vector.tensor_copy(late_picked[:], scale_table[:].indirect(own_sb[:, HALF // 16 : S // 16]))
         for j in range(4):
-            nc.sync.dma_start(own_plane[:].bitcast(I32)[OWN_ROW + j : P : 32, :], own_picked[:].bitcast(I32)[TABLE_ROW + 8 * j : P : 32, :])
+            nc.sync.dma_start(late_plane[:].bitcast(I32)[OWN_ROW + j : P : 32, :], late_picked[:].bitcast(I32)[TABLE_ROW + 8 * j : P : 32, :])
 
         head_words = keep.tile([P, S], U32, name="head_words", align_bytes=64)
         nc.vector.tensor_copy(head_words[:], word_table[:].indirect(offs_sb[:]))
 
-        e_banks = [psum.tile([P, HALF], F32, name="e%d" % i) for i in range(2 * m_tiles)]
+        def gather_own(tile, start, stop):
+            nc.vector.tensor_copy(tile[:], word_table[:].indirect(own_sb[:, start // 16 : stop // 16]))
+
+        own_first = keep.tile([P, PIECE], U32, name="own_first", align_bytes=64)
+        gather_own(own_first, 0, PIECE)
 
         w1_grouped = keep.tile([P, N, PACK], BF16, name="w1_grouped", align_bytes=64)
         cast(nc.scalar.copy, w1_grouped[:, 0:M_TILE, :], w1_raw[:, :, 0:M_TILE])
@@ -91,8 +97,8 @@ def tile_picked_phmix_silu_p_kernel(tc, x_words, x_scales, w1, w2, offs, own, ou
         cast(gpsimd_copy, w1_grouped[:, M_TILE + SCALAR_SHARE : N, :], w1_raw[:, :, M_TILE + SCALAR_SHARE : N])
         w1_q = [quantise("w1_0", w1_grouped[:, 0:M_TILE, :])]
         w1_q.append(quantise("w1_1", w1_grouped[:, M_TILE:N, :]))
-        own_words = [reuse.tile([P, HALF], U32, name="own_words0", offset=12288, align_bytes=64)]
-        nc.vector.tensor_copy(own_words[0][:], word_table[:].indirect(own_sb[:, 0 : HALF // 16]))
+        own_middle = reuse.tile([P, 2 * PIECE], U32, name="own_middle", offset=12288, align_bytes=64)
+        gather_own(own_middle, PIECE, 3 * PIECE)
 
         w2_grouped = [reuse.tile([P, M_TILE, PACK], BF16, name="w2_grouped%d" % mt, offset=8192 + 1024 * mt, align_bytes=64) for mt in range(m_tiles)]
         cast(nc.scalar.copy, w2_grouped[0][:], w2_raw[:, :, 0:M_TILE])
@@ -100,8 +106,8 @@ def tile_picked_phmix_silu_p_kernel(tc, x_words, x_scales, w1, w2, offs, own, ou
         cast(gpsimd_copy, w2_grouped[1][:, SCALAR_SHARE:M_TILE, :], w2_raw[:, :, M_TILE + SCALAR_SHARE : N])
         w2_q = [quantise("w2_0", w2_grouped[0][:])]
         w2_q.append(quantise("w2_1", w2_grouped[1][:]))
-        own_words.append(reuse.tile([P, HALF], U32, name="own_words1", offset=6144, align_bytes=64))
-        nc.vector.tensor_copy(own_words[1][:], word_table[:].indirect(own_sb[:, HALF // 16 : S // 16]))
+        own_last = reuse.tile([P, PIECE], U32, name="own_last", offset=6144, align_bytes=64)
+        gather_own(own_last, 3 * PIECE, S)
 
         gate = keep.tile([P, m_tiles, S], F32, name="gate", align_bytes=64)
         for h in range(2):
@@ -109,15 +115,19 @@ def tile_picked_phmix_silu_p_kernel(tc, x_words, x_scales, w1, w2, offs, own, ou
                 cols = slice(h * HALF, (h + 1) * HALF)
                 y = psum.tile([P, HALF], F32, name="y%d_%d" % (mt, h))
                 nc.tensor.matmul_mx(out=y[:], lhsT=w1_q[mt][0][:].bitcast(FP8X4), lhsT_scale=w1_q[mt][1][:],
-                                    rhs=head_words[:, cols].bitcast(FP8X4), rhs_scale=head_plane[:, cols], start=True, stop=True)
+                                    rhs=head_words[:, cols].bitcast(FP8X4), rhs_scale=early_plane[:, cols], start=True, stop=True)
                 nc.scalar.activation(gate[:, mt, cols], y[:], SILU)
 
+        own_words = [own_first[:], own_middle[:, 0:PIECE], own_middle[:, PIECE : 2 * PIECE], own_last[:]]
+        own_scales = [early_plane[:, S : S + PIECE], early_plane[:, S + PIECE : S + HALF],
+                      late_plane[OWN_ROW:P, 0:PIECE], late_plane[OWN_ROW:P, PIECE:HALF]]
         for h in range(2):
             for mt in range(m_tiles):
                 cols = slice(h * HALF, (h + 1) * HALF)
-                e = e_banks[2 * mt + h]
-                nc.tensor.matmul_mx(out=e[:], lhsT=w2_q[mt][0][:].bitcast(FP8X4), lhsT_scale=w2_q[mt][1][:],
-                                    rhs=own_words[h][:].bitcast(FP8X4), rhs_scale=own_plane[OWN_ROW:P, cols], start=True, stop=True)
+                e = psum.tile([P, HALF], F32, name="e%d_%d" % (mt, h))
+                for i in range(2):
+                    nc.tensor.matmul_mx(out=e[:, i * PIECE : (i + 1) * PIECE], lhsT=w2_q[mt][0][:].bitcast(FP8X4), lhsT_scale=w2_q[mt][1][:],
+                                        rhs=own_words[2 * h + i].bitcast(FP8X4), rhs_scale=own_scales[2 * h + i], start=True, stop=True)
                 res = keep.tile([P, HALF], F32, name="res%d_%d" % (mt, h))
                 nc.vector.tensor_tensor(res[:], e[:], gate[:, mt, cols], MULT)
                 nc.sync.dma_start(out[mt * M_TILE : (mt + 1) * M_TILE, cols], res[:])

@@ -20,7 +20,7 @@ P = 128
 PACK = 4
 M_TILE = 128
 HALF = S // 2
-SCALAR_SHARE = 48
+SCALAR_SHARE = 16
 FIRST_WORDS = 448
 TABLE_ROW = 4
 OWN_ROW = 8
@@ -59,8 +59,8 @@ def tile_picked_phmix_silu_p_kernel(tc, x_words, x_scales, w1, w2, offs, own, ou
         def cast(copy, grouped, raw):
             copy(grouped.rearrange("p (c i) t -> p c t i", i=4), raw.rearrange("p t (c i) -> p c t i", i=4))
 
-        def gpsimd_copy(dst, src):
-            nc.gpsimd.tensor_scalar(dst, src, 1.0, 0.0, MULT, ADD)
+        def gpsimd_cast(grouped, raw):
+            nc.gpsimd.tensor_scalar(grouped, raw.rearrange("p t c -> p c t"), 1.0, 0.0, MULT, ADD)
 
         def quantise(name, grouped):
             codes = keep.tile([P, grouped.shape[1]], U32, name=name + "_codes", align_bytes=64)
@@ -94,7 +94,7 @@ def tile_picked_phmix_silu_p_kernel(tc, x_words, x_scales, w1, w2, offs, own, ou
         w1_grouped = keep.tile([P, N, PACK], BF16, name="w1_grouped", align_bytes=64)
         cast(nc.scalar.copy, w1_grouped[:, 0:M_TILE, :], w1_raw[:, :, 0:M_TILE])
         cast(nc.scalar.copy, w1_grouped[:, M_TILE : M_TILE + SCALAR_SHARE, :], w1_raw[:, :, M_TILE : M_TILE + SCALAR_SHARE])
-        cast(gpsimd_copy, w1_grouped[:, M_TILE + SCALAR_SHARE : N, :], w1_raw[:, :, M_TILE + SCALAR_SHARE : N])
+        gpsimd_cast(w1_grouped[:, M_TILE + SCALAR_SHARE : N, :], w1_raw[:, :, M_TILE + SCALAR_SHARE : N])
         w1_q = [quantise("w1_0", w1_grouped[:, 0:M_TILE, :])]
         w1_q.append(quantise("w1_1", w1_grouped[:, M_TILE:N, :]))
         own_middle = reuse.tile([P, 2 * PIECE], U32, name="own_middle", offset=12288, align_bytes=64)
@@ -103,7 +103,7 @@ def tile_picked_phmix_silu_p_kernel(tc, x_words, x_scales, w1, w2, offs, own, ou
         w2_grouped = [reuse.tile([P, M_TILE, PACK], BF16, name="w2_grouped%d" % mt, offset=8192 + 1024 * mt, align_bytes=64) for mt in range(m_tiles)]
         cast(nc.scalar.copy, w2_grouped[0][:], w2_raw[:, :, 0:M_TILE])
         cast(nc.scalar.copy, w2_grouped[1][:, 0:SCALAR_SHARE, :], w2_raw[:, :, M_TILE : M_TILE + SCALAR_SHARE])
-        cast(gpsimd_copy, w2_grouped[1][:, SCALAR_SHARE:M_TILE, :], w2_raw[:, :, M_TILE + SCALAR_SHARE : N])
+        gpsimd_cast(w2_grouped[1][:, SCALAR_SHARE:M_TILE, :], w2_raw[:, :, M_TILE + SCALAR_SHARE : N])
         w2_q = [quantise("w2_0", w2_grouped[0][:])]
         w2_q.append(quantise("w2_1", w2_grouped[1][:]))
         own_last = reuse.tile([P, PIECE], U32, name="own_last", offset=6144, align_bytes=64)

@@ -20,7 +20,7 @@ P = 128
 PACK = 4
 M_TILE = 128
 HALF = S // 2
-SCALAR_SHARE = 16
+SCALAR_SHARE = 56
 FIRST_WORDS = 448
 TABLE_ROW = 4
 OWN_ROW = 8

@@ -20,7 +20,8 @@ P = 128
 PACK = 4
 M_TILE = 128
 HALF = S // 2
-SCALAR_SHARE = 56
+GPSIMD_FROM = 96
+GPSIMD_TO = 168
 FIRST_WORDS = 448
 TABLE_ROW = 4
 OWN_ROW = 8
@@ -91,21 +92,22 @@ def tile_picked_phmix_silu_p_kernel(tc, x_words, x_scales, w1, w2, offs, own, ou
         own_first = keep.tile([P, PIECE], U32, name="own_first", align_bytes=64)
         gather_own(own_first, 0, PIECE)
 
+        def round_weight(grouped, raw):
+            cast(nc.scalar.copy, grouped[:, 0:GPSIMD_FROM, :], raw[:, :, 0:GPSIMD_FROM])
+            gpsimd_cast(grouped[:, GPSIMD_FROM:GPSIMD_TO, :], raw[:, :, GPSIMD_FROM:GPSIMD_TO])
+            cast(nc.scalar.copy, grouped[:, GPSIMD_TO:N, :], raw[:, :, GPSIMD_TO:N])
+
         w1_grouped = keep.tile([P, N, PACK], BF16, name="w1_grouped", align_bytes=64)
-        cast(nc.scalar.copy, w1_grouped[:, 0:M_TILE, :], w1_raw[:, :, 0:M_TILE])
-        cast(nc.scalar.copy, w1_grouped[:, M_TILE : M_TILE + SCALAR_SHARE, :], w1_raw[:, :, M_TILE : M_TILE + SCALAR_SHARE])
-        gpsimd_cast(w1_grouped[:, M_TILE + SCALAR_SHARE : N, :], w1_raw[:, :, M_TILE + SCALAR_SHARE : N])
+        round_weight(w1_grouped, w1_raw)
         w1_q = [quantise("w1_0", w1_grouped[:, 0:M_TILE, :])]
         w1_q.append(quantise("w1_1", w1_grouped[:, M_TILE:N, :]))
         own_middle = reuse.tile([P, 2 * PIECE], U32, name="own_middle", offset=12288, align_bytes=64)
         gather_own(own_middle, PIECE, 3 * PIECE)
 
-        w2_grouped = [reuse.tile([P, M_TILE, PACK], BF16, name="w2_grouped%d" % mt, offset=8192 + 1024 * mt, align_bytes=64) for mt in range(m_tiles)]
-        cast(nc.scalar.copy, w2_grouped[0][:], w2_raw[:, :, 0:M_TILE])
-        cast(nc.scalar.copy, w2_grouped[1][:, 0:SCALAR_SHARE, :], w2_raw[:, :, M_TILE : M_TILE + SCALAR_SHARE])
-        gpsimd_cast(w2_grouped[1][:, SCALAR_SHARE:M_TILE, :], w2_raw[:, :, M_TILE + SCALAR_SHARE : N])
-        w2_q = [quantise("w2_0", w2_grouped[0][:])]
-        w2_q.append(quantise("w2_1", w2_grouped[1][:]))
+        w2_grouped = keep.tile([P, N, PACK], BF16, name="w2_grouped", align_bytes=64)
+        round_weight(w2_grouped, w2_raw)
+        w2_q = [quantise("w2_0", w2_grouped[:, 0:M_TILE, :])]
+        w2_q.append(quantise("w2_1", w2_grouped[:, M_TILE:N, :]))
         own_last = reuse.tile([P, PIECE], U32, name="own_last", offset=6144, align_bytes=64)
         gather_own(own_last, 3 * PIECE, S)
 

from contextlib import ExitStack

import concourse.mybir as mybir

K, T, S, N = 512, 2048, 512, 256
FLOPS = 2 * 2 * K * N * S

F32 = mybir.dt.float32
BF16 = mybir.dt.bfloat16
I32 = mybir.dt.int32
U32 = mybir.dt.uint32
U16 = mybir.dt.uint16
U8 = mybir.dt.uint8
FP8X4 = mybir.dt.float8_e4m3fn_x4
SILU = mybir.ActivationFunctionType.Silu
MULT = mybir.AluOpType.mult
ADD = mybir.AluOpType.add

P = 128
PACK = 4
M_TILE = 128
HALF = S // 2
GPSIMD_FROM = 96
GPSIMD_TO = 168
FIRST_WORDS = 448
TABLE_ROW = 4
OWN_ROW = 8
PIECE = 128


def tile_picked_phmix_silu_p_kernel(tc, x_words, x_scales, w1, w2, offs, own, out):
    nc = tc.nc
    m_tiles = N // M_TILE
    with ExitStack() as ctx:
        keep = ctx.enter_context(tc.tile_pool(name="keep", bufs=1))
        reuse = ctx.enter_context(tc.tile_pool(name="reuse", bufs=1))
        psum = ctx.enter_context(tc.psum_pool(name="psum", bufs=1))

        offs_sb = keep.tile([P, S // 16], U16, name="offs_sb")
        own_sb = keep.tile([P, S // 16], U16, name="own_sb")
        scale_table = keep.tile([P, T], U8, name="scale_table", align_bytes=64)
        word_table = keep.tile([P, T], U32, name="word_table", align_bytes=64)
        w1_raw = reuse.tile([P, PACK, N], F32, name="w1_raw", offset=12288, align_bytes=64)
        w2_raw = reuse.tile([P, PACK, N], F32, name="w2_raw", offset=4096, align_bytes=64)
        word_rows = x_words[0].rearrange("p c r -> p (c r)").bitcast(I32)
        nc.sync.dma_start(word_table[:, 0:FIRST_WORDS].bitcast(I32), word_rows[:, 0:FIRST_WORDS])
        nc.sync.dma_start(offs_sb[:], offs)
        nc.sync.dma_start(own_sb[:], own)
        table_rows = scale_table[:].bitcast(I32)
        nc.vector.memset(table_rows, 0)
        nc.sync.dma_start(table_rows[TABLE_ROW:P:8, :], x_scales[0].bitcast(I32))
        nc.sync.dma_start(word_table[:, FIRST_WORDS:T].bitcast(I32), word_rows[:, FIRST_WORDS:T])
        nc.sync.dma_start(w1_raw[:], w1.rearrange("(p j) n -> p j n", j=PACK))
        nc.sync.dma_start(w2_raw[:], w2.rearrange("(p j) n -> p j n", j=PACK))

        warm = keep.tile([P, 8], F32, name="warm")
        nc.vector.memset(warm[:, 0:1], 0.0)
        nc.scalar.activation(warm[:, 1:2], warm[:, 0:1], SILU)

        def cast(copy, grouped, raw):
            copy(grouped.rearrange("p (c i) t -> p c t i", i=4), raw.rearrange("p t (c i) -> p c t i", i=4))

        def gpsimd_cast(grouped, raw):
            nc.gpsimd.tensor_scalar(grouped, raw.rearrange("p t c -> p c t"), 1.0, 0.0, MULT, ADD)

        def quantise(name, grouped):
            codes = keep.tile([P, grouped.shape[1]], U32, name=name + "_codes", align_bytes=64)
            plane = keep.tile([P, grouped.shape[1]], U8, name=name + "_plane", align_bytes=64)
            nc.vector.quantize_mx(out=codes[:].bitcast(FP8X4), scales=plane[:], in_=grouped.rearrange("p c t -> p (c t)"))
            return codes, plane

        early_plane = keep.tile([P, S + HALF], U8, name="early_plane", align_bytes=64)
        nc.vector.memset(early_plane[:].bitcast(I32), 0)
        late_plane = keep.tile([P, HALF], U8, name="late_plane", align_bytes=64)
        nc.vector.memset(late_plane[:].bitcast(I32), 0)
        early_picked = keep.tile([P, S + HALF], U8, name="early_picked", align_bytes=64)
        nc.vector.tensor_copy(early_picked[:, 0:S], scale_table[:].indirect(offs_sb[:]))
        nc.vector.tensor_copy(early_picked[:, S : S + HALF], scale_table[:].indirect(own_sb[:, 0 : HALF // 16]))
        for j in range(4):
            nc.scalar.dma_start(early_plane[:].bitcast(I32)[j:P:32, :], early_picked[:].bitcast(I32)[TABLE_ROW + 8 * j : P : 32, :])
        late_picked = keep.tile([P, HALF], U8, name="late_picked", align_bytes=64)
        nc.vector.tensor_copy(late_picked[:], scale_table[:].indirect(own_sb[:, HALF // 16 : S // 16]))
        for j in range(4):
            nc.sync.dma_start(late_plane[:].bitcast(I32)[OWN_ROW + j : P : 32, :], late_picked[:].bitcast(I32)[TABLE_ROW + 8 * j : P : 32, :])

        head_words = keep.tile([P, S], U32, name="head_words", align_bytes=64)
        nc.vector.tensor_copy(head_words[:], word_table[:].indirect(offs_sb[:]))

        def gather_own(tile, start, stop):
            nc.vector.tensor_copy(tile[:], word_table[:].indirect(own_sb[:, start // 16 : stop // 16]))

        own_first = keep.tile([P, PIECE], U32, name="own_first", align_bytes=64)
        gather_own(own_first, 0, PIECE)

        def round_weight(grouped, raw):
            cast(nc.scalar.copy, grouped[:, 0:GPSIMD_FROM, :], raw[:, :, 0:GPSIMD_FROM])
            gpsimd_cast(grouped[:, GPSIMD_FROM:GPSIMD_TO, :], raw[:, :, GPSIMD_FROM:GPSIMD_TO])
            cast(nc.scalar.copy, grouped[:, GPSIMD_TO:N, :], raw[:, :, GPSIMD_TO:N])

        w1_grouped = keep.tile([P, N, PACK], BF16, name="w1_grouped", align_bytes=64)
        round_weight(w1_grouped, w1_raw)
        w1_q = [quantise("w1_0", w1_grouped[:, 0:M_TILE, :])]
        w1_q.append(quantise("w1_1", w1_grouped[:, M_TILE:N, :]))
        own_middle = reuse.tile([P, 2 * PIECE], U32, name="own_middle", offset=12288, align_bytes=64)
        gather_own(own_middle, PIECE, 3 * PIECE)

        w2_grouped = keep.tile([P, N, PACK], BF16, name="w2_grouped", align_bytes=64)
        round_weight(w2_grouped, w2_raw)
        w2_q = [quantise("w2_0", w2_grouped[:, 0:M_TILE, :])]
        w2_q.append(quantise("w2_1", w2_grouped[:, M_TILE:N, :]))
        own_last = reuse.tile([P, PIECE], U32, name="own_last", offset=6144, align_bytes=64)
        gather_own(own_last, 3 * PIECE, S)

        gate = keep.tile([P, m_tiles, S], F32, name="gate", align_bytes=64)
        for h in range(2):
            for mt in range(m_tiles):
                cols = slice(h * HALF, (h + 1) * HALF)
                y = psum.tile([P, HALF], F32, name="y%d_%d" % (mt, h))
                nc.tensor.matmul_mx(out=y[:], lhsT=w1_q[mt][0][:].bitcast(FP8X4), lhsT_scale=w1_q[mt][1][:],
                                    rhs=head_words[:, cols].bitcast(FP8X4), rhs_scale=early_plane[:, cols], start=True, stop=True)
                nc.scalar.activation(gate[:, mt, cols], y[:], SILU)

        own_words = [own_first[:], own_middle[:, 0:PIECE], own_middle[:, PIECE : 2 * PIECE], own_last[:]]
        own_scales = [early_plane[:, S : S + PIECE], early_plane[:, S + PIECE : S + HALF],
                      late_plane[OWN_ROW:P, 0:PIECE], late_plane[OWN_ROW:P, PIECE:HALF]]
        for h in range(2):
            for mt in range(m_tiles):
                cols = slice(h * HALF, (h + 1) * HALF)
                e = psum.tile([P, HALF], F32, name="e%d_%d" % (mt, h))
                for i in range(2):
                    nc.tensor.matmul_mx(out=e[:, i * PIECE : (i + 1) * PIECE], lhsT=w2_q[mt][0][:].bitcast(FP8X4), lhsT_scale=w2_q[mt][1][:],
                                        rhs=own_words[2 * h + i].bitcast(FP8X4), rhs_scale=own_scales[2 * h + i], start=True, stop=True)
                res = keep.tile([P, HALF], F32, name="res%d_%d" % (mt, h))
                nc.vector.tensor_tensor(res[:], e[:], gate[:, mt, cols], MULT)
                nc.sync.dma_start(out[mt * M_TILE : (mt + 1) * M_TILE, cols], res[:])
